import numpy as np
import ml_dtypes


def mxq(x, axis, fmt="e4m3"):
    dtype, down = {"e4m3": (ml_dtypes.float8_e4m3fn, 7), "e5m2": (ml_dtypes.float8_e5m2, 14)}[fmt]
    v = np.moveaxis(np.asarray(x, np.float32).astype(ml_dtypes.bfloat16).astype(np.float64), axis, -1)
    blocks = v.reshape(v.shape[:-1] + (-1, 32))
    amax = np.abs(blocks).max(-1, keepdims=True)
    byte = np.maximum(np.where(amax > 0, np.frexp(amax)[1] - 1 + 127, 0) - down, 1)
    scale = np.exp2(byte - 127.0)
    codes = (blocks / scale).astype(np.float32).astype(dtype).astype(np.float64)
    return np.moveaxis((codes * scale).reshape(v.shape), -1, axis)


WIDE = False


def mx_kscale(k):
    if not WIDE:
        return np.ones(k)
    levels = np.array([10, -10, 5, -5, 0])
    if k % 512:
        return np.exp2(np.random.permutation(np.resize(levels, k // 32))).repeat(32)
    a = np.empty((k // 512, 16))
    for p in range(k // 512):
        a[p, :8] = np.random.permutation(np.resize(levels, 8))
        for g in range(8):
            far = levels[np.abs(levels - a[p, g]) >= 10]
            a[p, g + 8] = far[np.random.randint(len(far))]
    return np.exp2(a.ravel()).repeat(32)


def f64(x):
    return np.asarray(x).astype(np.float64)


def striped(idx):
    return np.tile(idx.reshape(-1, 16).T, (8, 1)).astype(np.uint16)


def unstriped(offs):
    return offs[:16].T.reshape(-1).astype(np.int64)


def relu2(v):
    return np.maximum(v, 0.0) ** 2


K, T, E, C, N = 3072, 768, 2, 256, 128


def by_expert(wq, xq):
    return np.concatenate([wq[e].T @ xq[:, e * C:(e + 1) * C] for e in range(E)], axis=1)


def setup_inputs():
    n = np.random.standard_normal
    s = mx_kscale(K)[:, None]
    return {
        "xT": (n((K, T)) * s).astype(np.float32),
        "w": (n((E, K, N)) / np.sqrt(K) / s[None]).astype(np.float32),
        "b": (0.3 * n((N, E))).astype(np.float32),
        "gate": np.tile(np.random.uniform(0.2, 1.0, E * C), (N, 1)).astype(np.float32),
        "offs": striped(np.random.permutation(T)[:E * C]),
    }


def reference(xT, w, b, gate, offs):
    idx = unstriped(offs)
    xq = mxq(f64(xT)[:, idx], 0, "e4m3")
    y = by_expert(mxq(f64(w), 1, "e4m3"), xq)
    y = relu2(y + np.repeat(f64(b), C, axis=1))
    out = np.zeros((N, T))
    out[:, idx] = f64(gate) * y
    return out

@@ -1,0 +1,149 @@
+from contextlib import ExitStack
+
+import concourse.mybir as mybir
+
+K, T, E, C, N = 3072, 768, 2, 256, 128
+FLOPS = 2 * K * N * E * C
+
+F32 = mybir.dt.float32
+BF16 = mybir.dt.bfloat16
+U32 = mybir.dt.uint32
+U16 = mybir.dt.uint16
+U8 = mybir.dt.uint8
+FP8X4 = mybir.dt.float8_e4m3fn_x4
+MULT = mybir.AluOpType.mult
+RELU = mybir.ActivationFunctionType.Relu
+
+P = 128
+J = 4
+PASSES = K // (P * J)
+I = 4
+
+TAIL = [(0, 0, 2), (0, 2, 2), (0, 4, 2), (1, 0, 2), (1, 2, 2), (1, 4, 1), (1, 5, 1)]
+SHARES = [("vector", 512, 768), ("scalar", 0, 512)]
+LAST_SHARES = [("vector", 512, 768), ("scalar", 256, 512), ("scalar", 0, 256)]
+PLANES = [(0, 0), (0, 4), (0, 8), (0, 12), (1, 0), (1, 4)]
+
+
+def tile_routed_moe_kernel(tc, xT, w, b, gate, offs, out):
+    nc = tc.nc
+    x_rows = xT.rearrange("(g p j) t -> g p j t", p=P, j=J)
+    w_rows = w.rearrange("e (g p j) n -> e p g j n", p=P, j=J)
+
+    with ExitStack() as ctx:
+        keep = ctx.enter_context(tc.tile_pool(name="keep", bufs=1))
+        psum = ctx.enter_context(tc.psum_pool(name="psum", bufs=1))
+
+        offsets = keep.tile([P, E * C // 16], U16, name="offsets")
+        bias = keep.tile([P, E], F32, name="bias")
+        gates = keep.tile([P, E * C], F32, name="gates")
+        x_raw = {}
+        w_raw = {}
+        for e, g0, n in TAIL:
+            w_raw[(e, g0)] = keep.tile([P, n, J, N], F32, name=f"w_raw{e}_{g0}")
+
+        def load_w(e, g0, n):
+            nc.sync.dma_start(w_raw[(e, g0)][:], w_rows[e, :, g0:g0 + n, :, :])
+
+        for g in range(PASSES):
+            for engine, t0, t1 in SHARES if g < PASSES - 1 else LAST_SHARES:
+                x_raw[(g, t0)] = keep.tile([P, J, t1 - t0], F32, name=f"x_raw{g}_{t0}")
+                nc.sync.dma_start(x_raw[(g, t0)][:], x_rows[g, :, :, t0:t1])
+            if g == 0:
+                nc.sync.dma_start(offsets[:], offs)
+        nc.sync.dma_start(bias[:], b)
+        nc.sync.dma_start(gates[:], gate)
+        for chunk in TAIL:
+            load_w(*chunk)
+
+        x_scales = [keep.tile([P, T], U8, name=f"x_scales{i}", align_bytes=64) for i in range(2)]
+        for tile in x_scales:
+            nc.gpsimd.memset(tile[:], 0)
+        window = keep.tile([P, T], F32, name="window")
+        nc.gpsimd.memset(window[:], 0.0)
+
+        w_words = [keep.tile([P, PASSES, N], U32, name=f"w_words{e}", align_bytes=64) for e in range(E)]
+        w_scales = [keep.tile([P, PASSES, N], U8, name=f"w_scales{e}", align_bytes=64) for e in range(E)]
+
+        def lay(engine, out, in_):
+            out = out.rearrange("p (c i) j -> p c j i", i=I)
+            in_ = in_.rearrange("p j (c i) -> p c j i", i=I)
+            if engine == "scalar":
+                nc.scalar.copy(out, in_)
+            else:
+                nc.vector.tensor_copy(out, in_)
+
+        def quantise_w(e, g0, n, shares):
+            raw = w_raw[(e, g0)]
+            pairs = keep.tile([P, n, N, J], BF16, name=f"w_bf{e}_{g0}", align_bytes=64)
+            for c in range(n):
+                for engine, n0, n1 in shares[c % len(shares)]:
+                    lay(engine, pairs[:, c, n0:n1, :], raw[:, c, :, n0:n1])
+            nc.vector.quantize_mx(
+                out=w_words[e][:, g0:g0 + n, :].rearrange("p c n -> p (c n)").bitcast(FP8X4),
+                scales=w_scales[e][:, g0:g0 + n, :].rearrange("p c n -> p (c n)"),
+                in_=pairs[:].rearrange("p c n j -> p (c n j)"),
+            )
+
+        words = []
+        sums = [psum.tile([P, C], F32, name=f"sums{e}") for e in range(E)]
+        picked_scales = []
+
+        def gather_scales(i):
+            picked = keep.tile([P, E * C], U8, name=f"picked_scales{i}", align_bytes=64)
+            nc.vector.tensor_copy(picked[:], x_scales[i][:].indirect(offsets[:]))
+            picked_scales.append(picked)
+
+        def multiply(e, g):
+            cols = slice(e * C, (e + 1) * C)
+            i, k = PLANES[g]
+            nc.tensor.matmul_mx(
+                out=sums[e][:],
+                lhsT=w_words[e][:, g, :].bitcast(FP8X4),
+                lhsT_scale=w_scales[e][:, g, :],
+                rhs=words[g][:, cols].bitcast(FP8X4),
+                rhs_scale=picked_scales[i][k:P, cols],
+                start=(g == 0),
+                stop=(g == PASSES - 1),
+            )
+
+        for g in range(PASSES):
+            laid = keep.tile([P, T, J], BF16, name=f"x_bf{g}", align_bytes=64)
+            last = g == PASSES - 1
+            shares = LAST_SHARES if last else SHARES
+            for engine, t0, t1 in shares:
+                lay(engine, laid[:, t0:t1, :], x_raw[(g, t0)][:])
+            codes = keep.tile([P, T], U32, name=f"x_words{g}", align_bytes=64)
+            i, k = PLANES[g]
+            for engine, t0, t1 in shares:
+                nc.vector.quantize_mx(
+                    out=codes[:, t0:t1].bitcast(FP8X4),
+                    scales=x_scales[i][k:P, t0:t1],
+                    in_=laid[:, t0:t1, :].rearrange("p t j -> p (t j)"),
+                )
+            picked = keep.tile([P, E * C], U32, name=f"picked_words{g}", align_bytes=64)
+            nc.vector.tensor_copy(picked[:], codes[:].indirect(offsets[:]))
+            words.append(picked)
+            if g == 3:
+                gather_scales(0)
+        gather_scales(1)
+
+        def finish(e):
+            cols = slice(e * C, (e + 1) * C)
+            rectified = keep.tile([P, C], F32, name=f"rectified{e}")
+            squared = keep.tile([P, C], F32, name=f"squared{e}")
+            nc.scalar.activation(rectified[:], sums[e][:], RELU, bias=bias[:, e:e + 1])
+            nc.scalar.square(squared[:], rectified[:])
+            nc.vector.tensor_tensor(
+                window[:].indirect(offsets[:, e * C // 16:(e + 1) * C // 16]), squared[:], gates[:, cols], MULT
+            )
+
+        for chunk in TAIL:
+            e, g0, n = chunk
+            quantise_w(*chunk, [[("scalar", 0, 64), ("vector", 64, 128)]] if chunk == TAIL[-1] else [[("scalar", 0, 128)]])
+            for h in range(g0, g0 + n):
+                multiply(e, h)
+            if chunk[:2] == (0, 4):
+                finish(0)
+        finish(1)
+        nc.sync.dma_start(out, window[:])

@@ -16,13 +16,18 @@ RELU = mybir.ActivationFunctionType.Relu
 
 P = 128
 J = 4
-PASSES = K // (P * J)
 I = 4
+PASSES = K // (P * J)
 
-TAIL = [(0, 0, 2), (0, 2, 2), (0, 4, 2), (1, 0, 2), (1, 2, 2), (1, 4, 1), (1, 5, 1)]
-SHARES = [("vector", 512, 768), ("scalar", 0, 512)]
-LAST_SHARES = [("vector", 512, 768), ("scalar", 256, 512), ("scalar", 0, 256)]
-PLANES = [(0, 0), (0, 4), (0, 8), (0, 12), (1, 0), (1, 4)]
+LAST = PASSES - 1
+X_FIRST_CASTS = [("vector", 512, 768), ("scalar", 256, 384), ("vector", 384, 512), ("scalar", 0, 256)]
+X_CASTS = [("vector", 512, 768), ("scalar", 0, 512)]
+X_LAST_CASTS = [("vector", 512, 768), ("scalar", 256, 512), ("scalar", 0, 256)]
+X_QUANTS = [(512, 768), (0, 512)]
+X_LAST_QUANTS = [(512, 768), (256, 512), (0, 256)]
+W_CHUNKS = [(0, 0, 2), (0, 2, 2), (0, 4, 2), (1, 0, 2), (1, 2, 2), (1, 4, 1), (1, 5, 1)]
+W_SCALAR_COLUMNS = [[128, 128, 128, 128, 0, 128], [64, 128, 128, 0, 64, 64]]
+PLANES = [(0, 0), (0, 4), (1, 0), (1, 4), (1, 8), (1, 12)]
 
 
 def tile_routed_moe_kernel(tc, xT, w, b, gate, offs, out):
@@ -32,29 +37,12 @@ def tile_routed_moe_kernel(tc, xT, w, b, gate, offs, out):
 
     with ExitStack() as ctx:
         keep = ctx.enter_context(tc.tile_pool(name="keep", bufs=1))
+        pair = ctx.enter_context(tc.tile_pool(name="pair", bufs=2))
         psum = ctx.enter_context(tc.psum_pool(name="psum", bufs=1))
 
         offsets = keep.tile([P, E * C // 16], U16, name="offsets")
         bias = keep.tile([P, E], F32, name="bias")
         gates = keep.tile([P, E * C], F32, name="gates")
-        x_raw = {}
-        w_raw = {}
-        for e, g0, n in TAIL:
-            w_raw[(e, g0)] = keep.tile([P, n, J, N], F32, name=f"w_raw{e}_{g0}")
-
-        def load_w(e, g0, n):
-            nc.sync.dma_start(w_raw[(e, g0)][:], w_rows[e, :, g0:g0 + n, :, :])
-
-        for g in range(PASSES):
-            for engine, t0, t1 in SHARES if g < PASSES - 1 else LAST_SHARES:
-                x_raw[(g, t0)] = keep.tile([P, J, t1 - t0], F32, name=f"x_raw{g}_{t0}")
-                nc.sync.dma_start(x_raw[(g, t0)][:], x_rows[g, :, :, t0:t1])
-            if g == 0:
-                nc.sync.dma_start(offsets[:], offs)
-        nc.sync.dma_start(bias[:], b)
-        nc.sync.dma_start(gates[:], gate)
-        for chunk in TAIL:
-            load_w(*chunk)
 
         x_scales = [keep.tile([P, T], U8, name=f"x_scales{i}", align_bytes=64) for i in range(2)]
         for tile in x_scales:
@@ -64,6 +52,9 @@ def tile_routed_moe_kernel(tc, xT, w, b, gate, offs, out):
 
         w_words = [keep.tile([P, PASSES, N], U32, name=f"w_words{e}", align_bytes=64) for e in range(E)]
         w_scales = [keep.tile([P, PASSES, N], U8, name=f"w_scales{e}", align_bytes=64) for e in range(E)]
+        sums = [psum.tile([P, C], F32, name=f"sums{e}") for e in range(E)]
+        words = []
+        picked_scales = []
 
         def lay(engine, out, in_):
             out = out.rearrange("p (c i) j -> p c j i", i=I)
@@ -72,22 +63,6 @@ def tile_routed_moe_kernel(tc, xT, w, b, gate, offs, out):
                 nc.scalar.copy(out, in_)
             else:
                 nc.vector.tensor_copy(out, in_)
-
-        def quantise_w(e, g0, n, shares):
-            raw = w_raw[(e, g0)]
-            pairs = keep.tile([P, n, N, J], BF16, name=f"w_bf{e}_{g0}", align_bytes=64)
-            for c in range(n):
-                for engine, n0, n1 in shares[c % len(shares)]:
-                    lay(engine, pairs[:, c, n0:n1, :], raw[:, c, :, n0:n1])
-            nc.vector.quantize_mx(
-                out=w_words[e][:, g0:g0 + n, :].rearrange("p c n -> p (c n)").bitcast(FP8X4),
-                scales=w_scales[e][:, g0:g0 + n, :].rearrange("p c n -> p (c n)"),
-                in_=pairs[:].rearrange("p c n j -> p (c n j)"),
-            )
-
-        words = []
-        sums = [psum.tile([P, C], F32, name=f"sums{e}") for e in range(E)]
-        picked_scales = []
 
         def gather_scales(i):
             picked = keep.tile([P, E * C], U8, name=f"picked_scales{i}", align_bytes=64)
@@ -104,18 +79,20 @@ def tile_routed_moe_kernel(tc, xT, w, b, gate, offs, out):
                 rhs=words[g][:, cols].bitcast(FP8X4),
                 rhs_scale=picked_scales[i][k:P, cols],
                 start=(g == 0),
-                stop=(g == PASSES - 1),
+                stop=(g == LAST),
             )
 
         for g in range(PASSES):
-            laid = keep.tile([P, T, J], BF16, name=f"x_bf{g}", align_bytes=64)
-            last = g == PASSES - 1
-            shares = LAST_SHARES if last else SHARES
-            for engine, t0, t1 in shares:
-                lay(engine, laid[:, t0:t1, :], x_raw[(g, t0)][:])
+            raw = keep.tile([P, J, T], F32, name=f"x_raw{g}")
+            nc.sync.dma_start(raw[:], x_rows[g])
+            if g == 0:
+                nc.sync.dma_start(offsets[:], offs)
+            laid = pair.tile([P, T, J], BF16, name="laid", align_bytes=64)
+            for engine, t0, t1 in X_FIRST_CASTS if g == 0 else X_LAST_CASTS if g == LAST else X_CASTS:
+                lay(engine, laid[:, t0:t1, :], raw[:, :, t0:t1])
             codes = keep.tile([P, T], U32, name=f"x_words{g}", align_bytes=64)
             i, k = PLANES[g]
-            for engine, t0, t1 in shares:
+            for t0, t1 in X_LAST_QUANTS if g == LAST else X_QUANTS:
                 nc.vector.quantize_mx(
                     out=codes[:, t0:t1].bitcast(FP8X4),
                     scales=x_scales[i][k:P, t0:t1],
@@ -124,9 +101,11 @@ def tile_routed_moe_kernel(tc, xT, w, b, gate, offs, out):
             picked = keep.tile([P, E * C], U32, name=f"picked_words{g}", align_bytes=64)
             nc.vector.tensor_copy(picked[:], codes[:].indirect(offsets[:]))
             words.append(picked)
-            if g == 3:
+            if g == 1:
                 gather_scales(0)
         gather_scales(1)
+        nc.sync.dma_start(bias[:], b)
+        nc.sync.dma_start(gates[:], gate)
 
         def finish(e):
             cols = slice(e * C, (e + 1) * C)
@@ -138,12 +117,23 @@ def tile_routed_moe_kernel(tc, xT, w, b, gate, offs, out):
                 window[:].indirect(offsets[:, e * C // 16:(e + 1) * C // 16]), squared[:], gates[:, cols], MULT
             )
 
-        for chunk in TAIL:
-            e, g0, n = chunk
-            quantise_w(*chunk, [[("scalar", 0, 64), ("vector", 64, 128)]] if chunk == TAIL[-1] else [[("scalar", 0, 128)]])
-            for h in range(g0, g0 + n):
-                multiply(e, h)
-            if chunk[:2] == (0, 4):
-                finish(0)
-        finish(1)
+        for e, g0, n in W_CHUNKS:
+            raw = keep.tile([P, n, J, N], F32, name=f"w_raw{e}_{g0}")
+            nc.sync.dma_start(raw[:], w_rows[e, :, g0:g0 + n, :, :])
+            pairs = keep.tile([P, n, N, J], BF16, name=f"w_bf{e}_{g0}", align_bytes=64)
+            for c in range(n):
+                s = W_SCALAR_COLUMNS[e][g0 + c]
+                if s > 0:
+                    lay("scalar", pairs[:, c, 0:s, :], raw[:, c, :, 0:s])
+                if s < N:
+                    lay("vector", pairs[:, c, s:N, :], raw[:, c, :, s:N])
+            nc.vector.quantize_mx(
+                out=w_words[e][:, g0:g0 + n, :].rearrange("p c n -> p (c n)").bitcast(FP8X4),
+                scales=w_scales[e][:, g0:g0 + n, :].rearrange("p c n -> p (c n)"),
+                in_=pairs[:].rearrange("p c n j -> p (c n j)"),
+            )
+            for g in range(g0, g0 + n):
+                multiply(e, g)
+            if g0 + n == PASSES:
+                finish(e)
         nc.sync.dma_start(out, window[:])

@@ -20,13 +20,14 @@ I = 4
 PASSES = K // (P * J)
 
 LAST = PASSES - 1
-X_FIRST_CASTS = [("vector", 512, 768), ("scalar", 256, 384), ("vector", 384, 512), ("scalar", 0, 256)]
-X_CASTS = [("vector", 512, 768), ("scalar", 0, 512)]
-X_LAST_CASTS = [("vector", 512, 768), ("scalar", 256, 512), ("scalar", 0, 256)]
+X_LAST_LOADS = [(0, 512), (512, 768)]
+X_CASTS = [("gpsimd", 640, 768), ("vector", 512, 640), ("scalar", 0, 512)]
+X_LAST_CASTS = [("gpsimd", 640, 768), ("vector", 512, 640), ("vector", 448, 512), ("scalar", 0, 448)]
 X_QUANTS = [(512, 768), (0, 512)]
-X_LAST_QUANTS = [(512, 768), (256, 512), (0, 256)]
 W_CHUNKS = [(0, 0, 2), (0, 2, 2), (0, 4, 2), (1, 0, 2), (1, 2, 2), (1, 4, 1), (1, 5, 1)]
-W_SCALAR_COLUMNS = [[128, 128, 128, 128, 0, 128], [64, 128, 128, 0, 64, 64]]
+BOTH = [("gpsimd", 64, 128), ("scalar", 0, 64)]
+ALONE = [("scalar", 0, 128)]
+W_LAST = [("vector", 64, 128), ("scalar", 0, 64)]
 PLANES = [(0, 0), (0, 4), (1, 0), (1, 4), (1, 8), (1, 12)]
 
 
@@ -57,6 +58,9 @@ def tile_routed_moe_kernel(tc, xT, w, b, gate, offs, out):
         picked_scales = []
 
         def lay(engine, out, in_):
+            if engine == "gpsimd":
+                nc.gpsimd.tensor_copy(out, in_.rearrange("p j t -> p t j"))
+                return
             out = out.rearrange("p (c i) j -> p c j i", i=I)
             in_ = in_.rearrange("p j (c i) -> p c j i", i=I)
             if engine == "scalar":
@@ -83,16 +87,21 @@ def tile_routed_moe_kernel(tc, xT, w, b, gate, offs, out):
             )
 
         for g in range(PASSES):
-            raw = keep.tile([P, J, T], F32, name=f"x_raw{g}")
-            nc.sync.dma_start(raw[:], x_rows[g])
+            raws = []
+            for t0, t1 in X_LAST_LOADS if g == LAST else [(0, T)]:
+                raw = keep.tile([P, J, t1 - t0], F32, name=f"x_raw{g}_{t0}")
+                nc.sync.dma_start(raw[:], x_rows[g, :, :, t0:t1])
+                raws.append((t0, t1, raw))
             if g == 0:
                 nc.sync.dma_start(offsets[:], offs)
             laid = pair.tile([P, T, J], BF16, name="laid", align_bytes=64)
-            for engine, t0, t1 in X_FIRST_CASTS if g == 0 else X_LAST_CASTS if g == LAST else X_CASTS:
-                lay(engine, laid[:, t0:t1, :], raw[:, :, t0:t1])
+            for r0, r1, raw in raws:
+                for engine, t0, t1 in X_LAST_CASTS if g == LAST else X_CASTS:
+                    if r0 <= t0 < r1:
+                        lay(engine, laid[:, t0:t1, :], raw[:, :, t0 - r0:t1 - r0])
             codes = keep.tile([P, T], U32, name=f"x_words{g}", align_bytes=64)
             i, k = PLANES[g]
-            for t0, t1 in X_LAST_QUANTS if g == LAST else X_QUANTS:
+            for t0, t1 in X_QUANTS:
                 nc.vector.quantize_mx(
                     out=codes[:, t0:t1].bitcast(FP8X4),
                     scales=x_scales[i][k:P, t0:t1],
@@ -101,11 +110,10 @@ def tile_routed_moe_kernel(tc, xT, w, b, gate, offs, out):
             picked = keep.tile([P, E * C], U32, name=f"picked_words{g}", align_bytes=64)
             nc.vector.tensor_copy(picked[:], codes[:].indirect(offsets[:]))
             words.append(picked)
-            if g == 1:
+            if g == 2:
                 gather_scales(0)
         gather_scales(1)
         nc.sync.dma_start(bias[:], b)
-        nc.sync.dma_start(gates[:], gate)
 
         def finish(e):
             cols = slice(e * C, (e + 1) * C)
@@ -117,16 +125,20 @@ def tile_routed_moe_kernel(tc, xT, w, b, gate, offs, out):
                 window[:].indirect(offsets[:, e * C // 16:(e + 1) * C // 16]), squared[:], gates[:, cols], MULT
             )
 
+        w_raw = {}
         for e, g0, n in W_CHUNKS:
             raw = keep.tile([P, n, J, N], F32, name=f"w_raw{e}_{g0}")
             nc.sync.dma_start(raw[:], w_rows[e, :, g0:g0 + n, :, :])
+            w_raw[(e, g0)] = raw
+        nc.sync.dma_start(gates[:], gate)
+
+        for e, g0, n in W_CHUNKS:
+            raw = w_raw[(e, g0)]
             pairs = keep.tile([P, n, N, J], BF16, name=f"w_bf{e}_{g0}", align_bytes=64)
             for c in range(n):
-                s = W_SCALAR_COLUMNS[e][g0 + c]
-                if s > 0:
-                    lay("scalar", pairs[:, c, 0:s, :], raw[:, c, :, 0:s])
-                if s < N:
-                    lay("vector", pairs[:, c, s:N, :], raw[:, c, :, s:N])
+                shares = W_LAST if (e, g0) == (1, LAST) else BOTH if c == 0 else ALONE
+                for engine, n0, n1 in shares:
+                    lay(engine, pairs[:, c, n0:n1, :], raw[:, c, :, n0:n1])
             nc.vector.quantize_mx(
                 out=w_words[e][:, g0:g0 + n, :].rearrange("p c n -> p (c n)").bitcast(FP8X4),
                 scales=w_scales[e][:, g0:g0 + n, :].rearrange("p c n -> p (c n)"),

from contextlib import ExitStack

import concourse.mybir as mybir

K, T, E, C, N = 3072, 768, 2, 256, 128
FLOPS = 2 * K * N * E * C

F32 = mybir.dt.float32
BF16 = mybir.dt.bfloat16
U32 = mybir.dt.uint32
U16 = mybir.dt.uint16
U8 = mybir.dt.uint8
FP8X4 = mybir.dt.float8_e4m3fn_x4
MULT = mybir.AluOpType.mult
RELU = mybir.ActivationFunctionType.Relu

P = 128
J = 4
I = 4
PASSES = K // (P * J)

LAST = PASSES - 1
X_LAST_LOADS = [(0, 512), (512, 768)]
X_CASTS = [("gpsimd", 640, 768), ("vector", 512, 640), ("scalar", 0, 512)]
X_LAST_CASTS = [("gpsimd", 640, 768), ("vector", 512, 640), ("vector", 448, 512), ("scalar", 0, 448)]
X_QUANTS = [(512, 768), (0, 512)]
W_CHUNKS = [(0, 0, 2), (0, 2, 2), (0, 4, 2), (1, 0, 2), (1, 2, 2), (1, 4, 1), (1, 5, 1)]
BOTH = [("gpsimd", 64, 128), ("scalar", 0, 64)]
ALONE = [("scalar", 0, 128)]
W_LAST = [("vector", 64, 128), ("scalar", 0, 64)]
PLANES = [(0, 0), (0, 4), (1, 0), (1, 4), (1, 8), (1, 12)]


def tile_routed_moe_kernel(tc, xT, w, b, gate, offs, out):
    nc = tc.nc
    x_rows = xT.rearrange("(g p j) t -> g p j t", p=P, j=J)
    w_rows = w.rearrange("e (g p j) n -> e p g j n", p=P, j=J)

    with ExitStack() as ctx:
        keep = ctx.enter_context(tc.tile_pool(name="keep", bufs=1))
        pair = ctx.enter_context(tc.tile_pool(name="pair", bufs=2))
        psum = ctx.enter_context(tc.psum_pool(name="psum", bufs=1))

        offsets = keep.tile([P, E * C // 16], U16, name="offsets")
        bias = keep.tile([P, E], F32, name="bias")
        gates = keep.tile([P, E * C], F32, name="gates")

        x_scales = [keep.tile([P, T], U8, name=f"x_scales{i}", align_bytes=64) for i in range(2)]
        for tile in x_scales:
            nc.gpsimd.memset(tile[:], 0)
        window = keep.tile([P, T], F32, name="window")
        nc.gpsimd.memset(window[:], 0.0)

        w_words = [keep.tile([P, PASSES, N], U32, name=f"w_words{e}", align_bytes=64) for e in range(E)]
        w_scales = [keep.tile([P, PASSES, N], U8, name=f"w_scales{e}", align_bytes=64) for e in range(E)]
        sums = [psum.tile([P, C], F32, name=f"sums{e}") for e in range(E)]
        words = []
        picked_scales = []

        def lay(engine, out, in_):
            if engine == "gpsimd":
                nc.gpsimd.tensor_copy(out, in_.rearrange("p j t -> p t j"))
                return
            out = out.rearrange("p (c i) j -> p c j i", i=I)
            in_ = in_.rearrange("p j (c i) -> p c j i", i=I)
            if engine == "scalar":
                nc.scalar.copy(out, in_)
            else:
                nc.vector.tensor_copy(out, in_)

        def gather_scales(i):
            picked = keep.tile([P, E * C], U8, name=f"picked_scales{i}", align_bytes=64)
            nc.vector.tensor_copy(picked[:], x_scales[i][:].indirect(offsets[:]))
            picked_scales.append(picked)

        def multiply(e, g):
            cols = slice(e * C, (e + 1) * C)
            i, k = PLANES[g]
            nc.tensor.matmul_mx(
                out=sums[e][:],
                lhsT=w_words[e][:, g, :].bitcast(FP8X4),
                lhsT_scale=w_scales[e][:, g, :],
                rhs=words[g][:, cols].bitcast(FP8X4),
                rhs_scale=picked_scales[i][k:P, cols],
                start=(g == 0),
                stop=(g == LAST),
            )

        for g in range(PASSES):
            raws = []
            for t0, t1 in X_LAST_LOADS if g == LAST else [(0, T)]:
                raw = keep.tile([P, J, t1 - t0], F32, name=f"x_raw{g}_{t0}")
                nc.sync.dma_start(raw[:], x_rows[g, :, :, t0:t1])
                raws.append((t0, t1, raw))
            if g == 0:
                nc.sync.dma_start(offsets[:], offs)
            laid = pair.tile([P, T, J], BF16, name="laid", align_bytes=64)
            for r0, r1, raw in raws:
                for engine, t0, t1 in X_LAST_CASTS if g == LAST else X_CASTS:
                    if r0 <= t0 < r1:
                        lay(engine, laid[:, t0:t1, :], raw[:, :, t0 - r0:t1 - r0])
            codes = keep.tile([P, T], U32, name=f"x_words{g}", align_bytes=64)
            i, k = PLANES[g]
            for t0, t1 in X_QUANTS:
                nc.vector.quantize_mx(
                    out=codes[:, t0:t1].bitcast(FP8X4),
                    scales=x_scales[i][k:P, t0:t1],
                    in_=laid[:, t0:t1, :].rearrange("p t j -> p (t j)"),
                )
            picked = keep.tile([P, E * C], U32, name=f"picked_words{g}", align_bytes=64)
            nc.vector.tensor_copy(picked[:], codes[:].indirect(offsets[:]))
            words.append(picked)
            if g == 2:
                gather_scales(0)
        gather_scales(1)
        nc.sync.dma_start(bias[:], b)

        def finish(e):
            cols = slice(e * C, (e + 1) * C)
            rectified = keep.tile([P, C], F32, name=f"rectified{e}")
            squared = keep.tile([P, C], F32, name=f"squared{e}")
            nc.scalar.activation(rectified[:], sums[e][:], RELU, bias=bias[:, e:e + 1])
            nc.scalar.square(squared[:], rectified[:])
            nc.vector.tensor_tensor(
                window[:].indirect(offsets[:, e * C // 16:(e + 1) * C // 16]), squared[:], gates[:, cols], MULT
            )

        w_raw = {}
        for e, g0, n in W_CHUNKS:
            raw = keep.tile([P, n, J, N], F32, name=f"w_raw{e}_{g0}")
            nc.sync.dma_start(raw[:], w_rows[e, :, g0:g0 + n, :, :])
            w_raw[(e, g0)] = raw
        nc.sync.dma_start(gates[:], gate)

        for e, g0, n in W_CHUNKS:
            raw = w_raw[(e, g0)]
            pairs = keep.tile([P, n, N, J], BF16, name=f"w_bf{e}_{g0}", align_bytes=64)
            for c in range(n):
                shares = W_LAST if (e, g0) == (1, LAST) else BOTH if c == 0 else ALONE
                for engine, n0, n1 in shares:
                    lay(engine, pairs[:, c, n0:n1, :], raw[:, c, :, n0:n1])
            nc.vector.quantize_mx(
                out=w_words[e][:, g0:g0 + n, :].rearrange("p c n -> p (c n)").bitcast(FP8X4),
                scales=w_scales[e][:, g0:g0 + n, :].rearrange("p c n -> p (c n)"),
                in_=pairs[:].rearrange("p c n j -> p (c n j)"),
            )
            for g in range(g0, g0 + n):
                multiply(e, g)
            if g0 + n == PASSES:
                finish(e)
        nc.sync.dma_start(out, window[:])
